import numpy as np
import ml_dtypes


def mxq(x, axis, fmt="e4m3"):
    dtype, down = {"e4m3": (ml_dtypes.float8_e4m3fn, 7), "e5m2": (ml_dtypes.float8_e5m2, 14)}[fmt]
    v = np.moveaxis(np.asarray(x, np.float32).astype(ml_dtypes.bfloat16).astype(np.float64), axis, -1)
    blocks = v.reshape(v.shape[:-1] + (-1, 32))
    amax = np.abs(blocks).max(-1, keepdims=True)
    byte = np.maximum(np.where(amax > 0, np.frexp(amax)[1] - 1 + 127, 0) - down, 1)
    scale = np.exp2(byte - 127.0)
    codes = (blocks / scale).astype(np.float32).astype(dtype).astype(np.float64)
    return np.moveaxis((codes * scale).reshape(v.shape), -1, axis)


WIDE = False


def mx_kscale(k):
    if not WIDE:
        return np.ones(k)
    levels = np.array([10, -10, 5, -5, 0])
    if k % 512:
        return np.exp2(np.random.permutation(np.resize(levels, k // 32))).repeat(32)
    a = np.empty((k // 512, 16))
    for p in range(k // 512):
        a[p, :8] = np.random.permutation(np.resize(levels, 8))
        for g in range(8):
            far = levels[np.abs(levels - a[p, g]) >= 10]
            a[p, g + 8] = far[np.random.randint(len(far))]
    return np.exp2(a.ravel()).repeat(32)


def f64(x):
    return np.asarray(x).astype(np.float64)


def striped(idx):
    return np.tile(idx.reshape(-1, 16).T, (8, 1)).astype(np.uint16)


def unstriped(offs):
    return offs[:16].T.reshape(-1).astype(np.int64)


def pack_weight(w):
    k, n = w.shape
    w = f64(np.asarray(w, np.float32).astype(ml_dtypes.bfloat16)).reshape(k // 32, 32, n)
    amax = np.abs(w).max(1)
    byte = np.clip(np.where(amax > 0, np.frexp(amax)[1] - 1 + 127 - 7, 1), 1, 254)
    scaled = (w * np.exp2(127.0 - byte)[:, None, :]).reshape(k, n).astype(np.float32)
    words = np.ascontiguousarray(scaled.reshape(k // 512, 128, 4, n).transpose(0, 1, 3, 2)).astype(ml_dtypes.float8_e4m3fn).view(np.uint8)
    return words, np.ascontiguousarray(byte.astype(np.uint8).reshape(k // 512, 16, n))


def unpack_weight(words, scales):
    g, p, n, _ = words.shape
    vals = np.ascontiguousarray(words).view(ml_dtypes.float8_e4m3fn).astype(np.float64) * np.repeat(np.exp2(scales.astype(np.float64) - 127.0), 8, axis=1)[..., None]
    return vals.transpose(0, 1, 3, 2).reshape(g * 512, n)

def planes(y):
    n, m = y.shape
    v = y.astype(np.float32).astype(ml_dtypes.bfloat16).astype(np.float64).reshape(n // 32, 32, m)
    top = np.abs(v).max(1)
    byte = np.clip(np.where(top > 0, np.frexp(top)[1] - 1 + 127 - 7, 1), 1, 254)
    codes = (v * np.exp2(127.0 - byte)[:, None, :]).reshape(n, m).astype(np.float32).astype(ml_dtypes.float8_e4m3fn).view(np.uint8)
    words = codes.reshape(n // 512, 128, 4, m).transpose(0, 1, 3, 2)
    return np.ascontiguousarray(words), np.ascontiguousarray(byte.astype(np.uint8).reshape(n // 512, 16, m))


K, T, S, V, N = 512, 1024, 512, 128, 512


def setup_inputs():
    n = np.random.standard_normal
    s = mx_kscale(K)[:, None]
    packed_xT = pack_weight(n((K, T)) * s)
    return {
        "x_words": packed_xT[0],
        "x_scales": packed_xT[1],
        "w1": (n((K, N)) / np.sqrt(K) / s).astype(np.float32),
        "offs": striped(np.random.permutation(T)[:S]),
    }


def reference(x_words, x_scales, w1, offs):
    xq = unpack_weight(x_words, x_scales)[:, unstriped(offs)]
    e = np.exp(mxq(f64(w1), 0, "e4m3").T @ xq)
    out_0 = np.log(e[:, :V] + e[:, V:2 * V] + e[:, 2 * V:3 * V] + e[:, 3 * V:4 * V])
    return (out_0,) + planes(out_0)

@@ -1,0 +1,126 @@
+from contextlib import ExitStack
+
+import concourse.mybir as mybir
+from concourse.masks import make_identity
+
+F32 = mybir.dt.float32
+BF16 = mybir.dt.bfloat16
+I32 = mybir.dt.int32
+U32 = mybir.dt.uint32
+U16 = mybir.dt.uint16
+U8 = mybir.dt.uint8
+FP8X4 = mybir.dt.float8_e4m3fn_x4
+ACT = mybir.ActivationFunctionType
+ALU = mybir.AluOpType
+AX = mybir.AxisListType
+
+K, T, S, V, N = 512, 1024, 512, 128, 512
+D = S // V
+P = 128
+PACK = 4
+FLOPS = 2 * K * S * N
+
+
+def tile_picked_lsep_none_po_kernel(tc, x_words, x_scales, w1, offs, out_0, out_1, out_2):
+    nc = tc.nc
+    C = N // P
+    with ExitStack() as ctx:
+        keep = ctx.enter_context(tc.tile_pool(name="keep", bufs=1))
+        psum = ctx.enter_context(tc.psum_pool(name="psum", bufs=1))
+
+        offsets = keep.tile([P, S // 16], U16, name="offsets")
+        xw = keep.tile([P, T], I32, name="xw", align_bytes=64)
+        xs = keep.tile([P, T], U8, name="xs", align_bytes=64)
+        nc.vector.memset(xs[:, 0 : T // 2].bitcast(I32), 0)
+        nc.gpsimd.memset(xs[:, T // 2 :].bitcast(I32), 0)
+        nc.sync.dma_start(offsets[:], offs)
+        for q in range(4):
+            eng = nc.sync if q % 2 == 0 else nc.scalar
+            eng.dma_start(xs[32 * q : 32 * q + 4, :].bitcast(I32), x_scales[0, 4 * q : 4 * q + 4, :].bitcast(I32))
+        nc.sync.dma_start(xw[:], x_words[0].rearrange("p c r -> p (c r)").bitcast(I32))
+        w_rows = w1.rearrange("(p j) m -> p j m", j=PACK)
+        w_raw = [keep.tile([P, PACK, P], F32, name="w_raw%d" % c) for c in range(C)]
+        for c in range(C):
+            nc.sync.dma_start(w_raw[c][:], w_rows[:, :, c * P : (c + 1) * P])
+        ident = keep.tile([P, P], F32, name="ident")
+        make_identity(nc, ident[:])
+
+        gs = keep.tile([P, S], U8, name="gs", align_bytes=64)
+        nc.vector.tensor_copy(gs[:], xs[:].indirect(offsets[:]))
+        SH = S // 2
+        gw = [keep.tile([P, SH], U32, name="gw%d" % h, align_bytes=64) for h in range(2)]
+        for h in range(2):
+            nc.vector.tensor_copy(gw[h][:], xw[:].bitcast(U32).indirect(offsets[:, h * SH // 16 : (h + 1) * SH // 16]))
+
+        w_bf = [keep.tile([P, P, PACK], BF16, name="w_bf%d" % c, align_bytes=64) for c in range(C)]
+        wq = [keep.tile([P, P], U32, name="wq%d" % c, align_bytes=64) for c in range(C)]
+        ws = [keep.tile([P, P], U8, name="ws%d" % c, align_bytes=64) for c in range(C)]
+        y = [psum.tile([P, S], F32, name="y%d" % c, tag="y%d" % c) for c in range(C)]
+        for c in range(C):
+            nc.scalar.activation(w_bf[c][:].rearrange("p (a i) j -> p a j i", i=4),
+                                 w_raw[c][:].rearrange("p j (a i) -> p a j i", i=4), ACT.Copy)
+            nc.vector.quantize_mx(out=wq[c][:].bitcast(FP8X4), scales=ws[c][:],
+                                  in_=w_bf[c][:].rearrange("p m j -> p (m j)"))
+            for h in range(2):
+                cols = slice(h * SH, (h + 1) * SH)
+                nc.tensor.matmul_mx(out=y[c][:, cols], lhsT=wq[c][:].bitcast(FP8X4), lhsT_scale=ws[c][:],
+                                    rhs=gw[h][:].bitcast(FP8X4), rhs_scale=gs[:, cols], start=True, stop=True)
+
+        top = [keep.tile([P, V], F32, name="top%d" % c) for c in range(C)]
+        z = [keep.tile([P, D, V], F32, name="z%d" % c) for c in range(C)]
+        e = [keep.tile([P, D, V], F32, name="e%d" % c) for c in range(C)]
+        top_t = psum.tile([P, C, P], F32, name="top_t")
+        sum_ta = psum.tile([P, C - 1, P], F32, name="sum_ta")
+        sum_t = [sum_ta[:, c, :] for c in range(C - 1)]
+        for c in range(C):
+            nc.vector.tensor_reduce(top[c][:], y[c][:].rearrange("p (d v) -> p v d", d=D), AX.X, ALU.max)
+            nc.vector.tensor_tensor(z[c][:], y[c][:].rearrange("p (d v) -> p d v", d=D),
+                                    top[c][:].unsqueeze(1).to_broadcast([P, D, V]), ALU.subtract)
+            nc.tensor.transpose(top_t[:, c, :], top[c][:], ident[:])
+            if c == C - 1:
+                sum_tb = psum.tile([P, S], F32, name="sum_tb", tag="y0")
+                sum_t.append(sum_tb[:, 0:P])
+                pieces = ((0, 2), (2, 4))
+            else:
+                pieces = ((0, 4),)
+            for a, b in pieces:
+                nc.scalar.activation(e[c][:, a:b, :], z[c][:, a:b, :], ACT.Exp)
+                for d in range(a, b):
+                    nc.tensor.matmul(sum_t[c], e[c][:, d, :], ident[:], start=(d == 0), stop=(d == D - 1), is_transpose=True)
+
+        top_sb = keep.tile([P, PACK, P], F32, name="top_sb")
+        sum_sb = keep.tile([P, PACK, P], F32, name="sum_sb")
+        LC = P // PACK
+        nc.vector.tensor_copy(top_sb[:], top_t[:].rearrange("p c (i t) -> p t (c i)", t=PACK))
+        nc.vector.tensor_copy(sum_sb[:, :, 0 : (C - 1) * LC], sum_ta[:].rearrange("p c (i t) -> p t (c i)", t=PACK))
+        nc.vector.tensor_copy(sum_sb[:, :, (C - 1) * LC :], sum_t[C - 1].rearrange("p (i t) -> p t i", t=PACK))
+        top_d = psum.tile([P, PACK, V], F32, name="top_d", tag="y0")
+        sum_d = psum.tile([P, PACK, V], F32, name="sum_d")
+        for t in range(PACK):
+            nc.tensor.transpose(sum_d[:, t, :], sum_sb[:, t, :], ident[:])
+        for t in range(PACK):
+            nc.tensor.transpose(top_d[:, t, :], top_sb[:, t, :], ident[:])
+
+        VH = V // 2
+        logs = [keep.tile([P, PACK, VH], F32, name="logs%d" % g) for g in range(2)]
+        res = keep.tile([P, PACK, V], F32, name="res")
+        res_bf = [keep.tile([P, VH, PACK], BF16, name="res_bf%d" % g, align_bytes=64) for g in range(2)]
+        oq = keep.tile([P, V], U32, name="oq", align_bytes=64)
+        osc = keep.tile([P, V], U8, name="osc", align_bytes=64)
+        for g in range(2):
+            cols = slice(g * VH, (g + 1) * VH)
+            nc.scalar.activation(logs[g][:], sum_d[:, :, cols], ACT.Ln)
+            nc.vector.tensor_tensor(res[:, :, cols], top_d[:, :, cols], logs[g][:], ALU.add)
+        nc.sync.dma_start(out_0.rearrange("(p t) v -> p t v", t=PACK), res[:])
+        for g in range(2):
+            cols = slice(g * VH, (g + 1) * VH)
+            nc.scalar.activation(res_bf[g][:].rearrange("p (c i) t -> p c t i", i=4),
+                                 res[:, :, cols].rearrange("p t (c i) -> p c t i", i=4), ACT.Copy)
+        for g in range(2):
+            cols = slice(g * VH, (g + 1) * VH)
+            nc.vector.quantize_mx(out=oq[:, cols].bitcast(FP8X4), scales=osc[:, cols],
+                                  in_=res_bf[g][:].rearrange("p v t -> p (v t)"))
+        nc.sync.dma_start(out_1[0].rearrange("p c r -> p (c r)").bitcast(I32), oq[:].bitcast(I32))
+        for q in range(4):
+            eng = nc.scalar if q % 2 == 0 else nc.sync
+            eng.dma_start(out_2[0, 4 * q : 4 * q + 4, :].bitcast(I32), osc[32 * q : 32 * q + 4, :].bitcast(I32))

@@ -31,75 +31,95 @@ def tile_picked_lsep_none_po_kernel(tc, x_words, x_scales, w1, offs, out_0, out_
         offsets = keep.tile([P, S // 16], U16, name="offsets")
         xw = keep.tile([P, T], I32, name="xw", align_bytes=64)
         xs = keep.tile([P, T], U8, name="xs", align_bytes=64)
-        nc.vector.memset(xs[:, 0 : T // 2].bitcast(I32), 0)
-        nc.gpsimd.memset(xs[:, T // 2 :].bitcast(I32), 0)
+        nc.vector.memset(xs[:].bitcast(I32), 0)
+        w_rows = w1.rearrange("(p j) m -> p j m", j=PACK)
+        w_raw = [keep.tile([P, PACK, P], F32, name="w_raw%d" % c) for c in range(C)]
         nc.sync.dma_start(offsets[:], offs)
+        nc.sync.dma_start(w_raw[0][:], w_rows[:, :, 0:P])
         for q in range(4):
             eng = nc.sync if q % 2 == 0 else nc.scalar
             eng.dma_start(xs[32 * q : 32 * q + 4, :].bitcast(I32), x_scales[0, 4 * q : 4 * q + 4, :].bitcast(I32))
         nc.sync.dma_start(xw[:], x_words[0].rearrange("p c r -> p (c r)").bitcast(I32))
-        w_rows = w1.rearrange("(p j) m -> p j m", j=PACK)
-        w_raw = [keep.tile([P, PACK, P], F32, name="w_raw%d" % c) for c in range(C)]
-        for c in range(C):
+        for c in range(1, C):
             nc.sync.dma_start(w_raw[c][:], w_rows[:, :, c * P : (c + 1) * P])
         ident = keep.tile([P, P], F32, name="ident")
         make_identity(nc, ident[:])
 
         gs = keep.tile([P, S], U8, name="gs", align_bytes=64)
         nc.vector.tensor_copy(gs[:], xs[:].indirect(offsets[:]))
-        SH = S // 2
-        gw = [keep.tile([P, SH], U32, name="gw%d" % h, align_bytes=64) for h in range(2)]
-        for h in range(2):
-            nc.vector.tensor_copy(gw[h][:], xw[:].bitcast(U32).indirect(offsets[:, h * SH // 16 : (h + 1) * SH // 16]))
+        gw = keep.tile([P, S], U32, name="gw", align_bytes=64)
+        for a, b in ((0, S - V), (S - V, S)):
+            nc.vector.tensor_copy(gw[:, a:b], xw[:].bitcast(U32).indirect(offsets[:, a // 16 : b // 16]))
 
-        w_bf = [keep.tile([P, P, PACK], BF16, name="w_bf%d" % c, align_bytes=64) for c in range(C)]
+        w_bf = [keep.tile([P, P, PACK], BF16, name="w_bf%d" % c, tag="w_bf%d" % c, align_bytes=64) for c in range(C)]
         wq = [keep.tile([P, P], U32, name="wq%d" % c, align_bytes=64) for c in range(C)]
         ws = [keep.tile([P, P], U8, name="ws%d" % c, align_bytes=64) for c in range(C)]
         y = [psum.tile([P, S], F32, name="y%d" % c, tag="y%d" % c) for c in range(C)]
-        for c in range(C):
+        top = {}
+        z = {}
+        e = [keep.tile([P, D, V], F32, name="e%d" % c) for c in range(C)]
+        top_t = {}
+        sum_ta = psum.tile([P, C - 1, P], F32, name="sum_ta")
+
+        def cast(c):
             nc.scalar.activation(w_bf[c][:].rearrange("p (a i) j -> p a j i", i=4),
                                  w_raw[c][:].rearrange("p j (a i) -> p a j i", i=4), ACT.Copy)
+
+        def product(c):
             nc.vector.quantize_mx(out=wq[c][:].bitcast(FP8X4), scales=ws[c][:],
                                   in_=w_bf[c][:].rearrange("p m j -> p (m j)"))
-            for h in range(2):
-                cols = slice(h * SH, (h + 1) * SH)
+            for a, b in ((0, 2 * V), (2 * V, 3 * V), (3 * V, S)) if c == 0 else ((0, S),):
+                cols = slice(a, b)
                 nc.tensor.matmul_mx(out=y[c][:, cols], lhsT=wq[c][:].bitcast(FP8X4), lhsT_scale=ws[c][:],
-                                    rhs=gw[h][:].bitcast(FP8X4), rhs_scale=gs[:, cols], start=True, stop=True)
+                                    rhs=gw[:, cols].bitcast(FP8X4), rhs_scale=gs[:, cols], start=True, stop=True)
 
-        top = [keep.tile([P, V], F32, name="top%d" % c) for c in range(C)]
-        z = [keep.tile([P, D, V], F32, name="z%d" % c) for c in range(C)]
-        e = [keep.tile([P, D, V], F32, name="e%d" % c) for c in range(C)]
-        top_t = psum.tile([P, C, P], F32, name="top_t")
-        sum_ta = psum.tile([P, C - 1, P], F32, name="sum_ta")
-        sum_t = [sum_ta[:, c, :] for c in range(C - 1)]
-        for c in range(C):
+        def largest(c):
+            top[c] = keep.tile([P, V], F32, name="top%d" % c, tag="w_bf1" if c == 0 else "top%d" % c, align_bytes=64)
             nc.vector.tensor_reduce(top[c][:], y[c][:].rearrange("p (d v) -> p v d", d=D), AX.X, ALU.max)
-            nc.vector.tensor_tensor(z[c][:], y[c][:].rearrange("p (d v) -> p d v", d=D),
-                                    top[c][:].unsqueeze(1).to_broadcast([P, D, V]), ALU.subtract)
-            nc.tensor.transpose(top_t[:, c, :], top[c][:], ident[:])
-            if c == C - 1:
-                sum_tb = psum.tile([P, S], F32, name="sum_tb", tag="y0")
-                sum_t.append(sum_tb[:, 0:P])
-                pieces = ((0, 2), (2, 4))
-            else:
-                pieces = ((0, 4),)
+            if c % 2 == 0:
+                top_t[c // 2] = psum.tile([P, C, P], F32, name="top_t%d" % c, tag="top_t" if c == 0 else "y0")
+            nc.tensor.transpose(top_t[c // 2][:, c % 2, :], top[c][:], ident[:])
+
+        def exp_sum(c, sums, pieces):
+            z[c] = keep.tile([P, D, V], F32, name="z%d" % c, tag="w_bf2" if c == 0 else "z%d" % c, align_bytes=64)
             for a, b in pieces:
+                nc.vector.tensor_tensor(z[c][:, a:b, :], y[c][:].rearrange("p (d v) -> p d v", d=D)[:, a:b, :],
+                                        top[c][:].unsqueeze(1).to_broadcast([P, b - a, V]), ALU.subtract)
                 nc.scalar.activation(e[c][:, a:b, :], z[c][:, a:b, :], ACT.Exp)
                 for d in range(a, b):
-                    nc.tensor.matmul(sum_t[c], e[c][:, d, :], ident[:], start=(d == 0), stop=(d == D - 1), is_transpose=True)
+                    nc.tensor.matmul(sums, e[c][:, d, :], ident[:], start=(d == 0), stop=(d == D - 1), is_transpose=True)
 
         top_sb = keep.tile([P, PACK, P], F32, name="top_sb")
         sum_sb = keep.tile([P, PACK, P], F32, name="sum_sb")
         LC = P // PACK
-        nc.vector.tensor_copy(top_sb[:], top_t[:].rearrange("p c (i t) -> p t (c i)", t=PACK))
-        nc.vector.tensor_copy(sum_sb[:, :, 0 : (C - 1) * LC], sum_ta[:].rearrange("p c (i t) -> p t (c i)", t=PACK))
-        nc.vector.tensor_copy(sum_sb[:, :, (C - 1) * LC :], sum_t[C - 1].rearrange("p (i t) -> p t i", t=PACK))
-        top_d = psum.tile([P, PACK, V], F32, name="top_d", tag="y0")
+
+        def deal(dst, src, a, b):
+            nc.vector.tensor_copy(dst[:, :, a * LC : b * LC], src.rearrange("p c (i t) -> p t (c i)", t=PACK))
+
+        for c in range(C):
+            cast(c)
+        product(0)
+        product(1)
+        largest(0)
+        product(2)
+        exp_sum(0, sum_ta[:, 0, :], ((0, D),))
+        product(3)
+        largest(1)
+        largest(2)
+        exp_sum(1, sum_ta[:, 1, :], ((0, D),))
+        exp_sum(2, sum_ta[:, 2, :], ((0, D),))
+        largest(3)
+        deal(top_sb, top_t[0][:, 0:2, :], 0, 2)
+        sum_tb = psum.tile([P, C, P], F32, name="sum_tb", tag="y1")
+        exp_sum(3, sum_tb[:, 0, :], ((0, 2), (2, D)))
+        deal(sum_sb, sum_ta[:], 0, C - 1)
+        deal(top_sb, top_t[1][:, 0:2, :], 2, C)
+        deal(sum_sb, sum_tb[:, 0:1, :], C - 1, C)
+        top_d = psum.tile([P, PACK, V], F32, name="top_d")
         sum_d = psum.tile([P, PACK, V], F32, name="sum_d")
-        for t in range(PACK):
-            nc.tensor.transpose(sum_d[:, t, :], sum_sb[:, t, :], ident[:])
-        for t in range(PACK):
-            nc.tensor.transpose(top_d[:, t, :], top_sb[:, t, :], ident[:])
+        for src, dst in ((top_sb, top_d), (sum_sb, sum_d)):
+            for t in range(PACK):
+                nc.tensor.transpose(dst[:, t, :], src[:, t, :], ident[:])
 
         VH = V // 2
         logs = [keep.tile([P, PACK, VH], F32, name="logs%d" % g) for g in range(2)]

@@ -47,79 +47,90 @@ def tile_picked_lsep_none_po_kernel(tc, x_words, x_scales, w1, offs, out_0, out_
 
         gs = keep.tile([P, S], U8, name="gs", align_bytes=64)
         nc.vector.tensor_copy(gs[:], xs[:].indirect(offsets[:]))
-        gw = keep.tile([P, S], U32, name="gw", align_bytes=64)
-        for a, b in ((0, S - V), (S - V, S)):
-            nc.vector.tensor_copy(gw[:, a:b], xw[:].bitcast(U32).indirect(offsets[:, a // 16 : b // 16]))
-
         w_bf = [keep.tile([P, P, PACK], BF16, name="w_bf%d" % c, tag="w_bf%d" % c, align_bytes=64) for c in range(C)]
         wq = [keep.tile([P, P], U32, name="wq%d" % c, align_bytes=64) for c in range(C)]
         ws = [keep.tile([P, P], U8, name="ws%d" % c, align_bytes=64) for c in range(C)]
         y = [psum.tile([P, S], F32, name="y%d" % c, tag="y%d" % c) for c in range(C)]
-        top = {}
-        z = {}
-        e = [keep.tile([P, D, V], F32, name="e%d" % c) for c in range(C)]
-        top_t = {}
-        sum_ta = psum.tile([P, C - 1, P], F32, name="sum_ta")
+        LC = P // PACK
 
         def cast(c):
             nc.scalar.activation(w_bf[c][:].rearrange("p (a i) j -> p a j i", i=4),
                                  w_raw[c][:].rearrange("p j (a i) -> p a j i", i=4), ACT.Copy)
 
-        def product(c):
+        def quantise(c):
             nc.vector.quantize_mx(out=wq[c][:].bitcast(FP8X4), scales=ws[c][:],
                                   in_=w_bf[c][:].rearrange("p m j -> p (m j)"))
-            for a, b in ((0, 2 * V), (2 * V, 3 * V), (3 * V, S)) if c == 0 else ((0, S),):
-                cols = slice(a, b)
-                nc.tensor.matmul_mx(out=y[c][:, cols], lhsT=wq[c][:].bitcast(FP8X4), lhsT_scale=ws[c][:],
-                                    rhs=gw[:, cols].bitcast(FP8X4), rhs_scale=gs[:, cols], start=True, stop=True)
 
-        def largest(c):
-            top[c] = keep.tile([P, V], F32, name="top%d" % c, tag="w_bf1" if c == 0 else "top%d" % c, align_bytes=64)
-            nc.vector.tensor_reduce(top[c][:], y[c][:].rearrange("p (d v) -> p v d", d=D), AX.X, ALU.max)
-            if c % 2 == 0:
-                top_t[c // 2] = psum.tile([P, C, P], F32, name="top_t%d" % c, tag="top_t" if c == 0 else "y0")
-            nc.tensor.transpose(top_t[c // 2][:, c % 2, :], top[c][:], ident[:])
+        def product(c):
+            for d in range(D):
+                cols = slice(d * V, (d + 1) * V)
+                nc.tensor.matmul_mx(out=y[c][:, cols], lhsT=gw[:, cols].bitcast(FP8X4), lhsT_scale=gs[:, cols],
+                                    rhs=wq[c][:].bitcast(FP8X4), rhs_scale=ws[c][:], start=True, stop=True)
 
-        def exp_sum(c, sums, pieces):
-            z[c] = keep.tile([P, D, V], F32, name="z%d" % c, tag="w_bf2" if c == 0 else "z%d" % c, align_bytes=64)
+        def largest(c, pieces):
+            scores = y[c][:].rearrange("p (d i t) -> p t i d", d=D, t=PACK)
             for a, b in pieces:
-                nc.vector.tensor_tensor(z[c][:, a:b, :], y[c][:].rearrange("p (d v) -> p d v", d=D)[:, a:b, :],
-                                        top[c][:].unsqueeze(1).to_broadcast([P, b - a, V]), ALU.subtract)
-                nc.scalar.activation(e[c][:, a:b, :], z[c][:, a:b, :], ACT.Exp)
-                for d in range(a, b):
-                    nc.tensor.matmul(sums, e[c][:, d, :], ident[:], start=(d == 0), stop=(d == D - 1), is_transpose=True)
+                nc.vector.tensor_reduce(top_sb[:, a:b, c * LC : (c + 1) * LC], scores[:, a:b, :, :], AX.X, ALU.max)
 
-        top_sb = keep.tile([P, PACK, P], F32, name="top_sb")
-        sum_sb = keep.tile([P, PACK, P], F32, name="sum_sb")
-        LC = P // PACK
+        def exp_sum_gpsimd(c):
+            z = keep.tile([P, D, PACK, LC], F32, name="z%d" % c, tag="w_bf2" if c == 0 else "z%d" % c, align_bytes=64)
+            e = keep.tile([P, D, PACK, LC], F32, name="e%d" % c)
+            pair = keep.tile([P, 2, PACK, LC], F32, name="pair%d" % c)
+            shift = top_sb[:, :, c * LC : (c + 1) * LC].unsqueeze(1).to_broadcast([P, D, PACK, LC])
+            nc.vector.tensor_tensor(z[:], y[c][:].rearrange("p (d i t) -> p d t i", d=D, t=PACK), shift, ALU.subtract)
+            nc.scalar.activation(e[:], z[:], ACT.Exp)
+            nc.gpsimd.tensor_tensor(pair[:], e[:, 0:2, :, :], e[:, 2:4, :, :], ALU.add)
+            for u in range(2):
+                nc.gpsimd.tensor_tensor(sum_sb[u][:, :, c * LC : (c + 1) * LC], pair[:, 0, 2 * u : 2 * u + 2, :],
+                                        pair[:, 1, 2 * u : 2 * u + 2, :], ALU.add)
 
-        def deal(dst, src, a, b):
-            nc.vector.tensor_copy(dst[:, :, a * LC : b * LC], src.rearrange("p c (i t) -> p t (c i)", t=PACK))
+        def exp_vector(c, pieces):
+            z = keep.tile([P, PACK, LC, D], F32, name="z%d" % c)
+            e = keep.tile([P, PACK, LC, D], F32, name="e%d" % c)
+            scores = y[c][:].rearrange("p (d i t) -> p t i d", d=D, t=PACK)
+            for a, b in pieces:
+                shift = top_sb[:, a:b, c * LC : (c + 1) * LC].unsqueeze(3).to_broadcast([P, b - a, LC, D])
+                nc.vector.tensor_tensor(z[:, a:b, :, :], scores[:, a:b, :, :], shift, ALU.subtract)
+                nc.scalar.activation(e[:, a:b, :, :], z[:, a:b, :, :], ACT.Exp)
+            return e
 
-        for c in range(C):
-            cast(c)
-        product(0)
-        product(1)
-        largest(0)
-        product(2)
-        exp_sum(0, sum_ta[:, 0, :], ((0, D),))
-        product(3)
-        largest(1)
-        largest(2)
-        exp_sum(1, sum_ta[:, 1, :], ((0, D),))
-        exp_sum(2, sum_ta[:, 2, :], ((0, D),))
-        largest(3)
-        deal(top_sb, top_t[0][:, 0:2, :], 0, 2)
-        sum_tb = psum.tile([P, C, P], F32, name="sum_tb", tag="y1")
-        exp_sum(3, sum_tb[:, 0, :], ((0, 2), (2, D)))
-        deal(sum_sb, sum_ta[:], 0, C - 1)
-        deal(top_sb, top_t[1][:, 0:2, :], 2, C)
-        deal(sum_sb, sum_tb[:, 0:1, :], C - 1, C)
+        def sum_vector(c, e, u):
+            nc.vector.tensor_reduce(sum_sb[u][:, :, c * LC : (c + 1) * LC], e[:, 2 * u : 2 * u + 2, :, :], AX.X, ALU.add)
+
+        sum_sb = [keep.tile([P, 2, P], F32, name="sum_sb%d" % u) for u in range(2)]
+        whole, halves = ((0, PACK),), ((0, 2), (2, PACK))
         top_d = psum.tile([P, PACK, V], F32, name="top_d")
         sum_d = psum.tile([P, PACK, V], F32, name="sum_d")
-        for src, dst in ((top_sb, top_d), (sum_sb, sum_d)):
-            for t in range(PACK):
-                nc.tensor.transpose(dst[:, t, :], src[:, t, :], ident[:])
+        for c in range(C):
+            cast(c)
+        quantise(0)
+        gw = keep.tile([P, S], U32, name="gw", align_bytes=64)
+        for a, b in ((0, 2 * V), (2 * V, 3 * V), (3 * V, S)):
+            nc.vector.tensor_copy(gw[:, a:b], xw[:].bitcast(U32).indirect(offsets[:, a // 16 : b // 16]))
+        product(0)
+        quantise(1)
+        product(1)
+        top_sb = keep.tile([P, PACK, P], F32, name="top_sb", tag="w_bf1", align_bytes=64)
+        largest(0, whole)
+        quantise(2)
+        product(2)
+        exp_sum_gpsimd(0)
+        quantise(3)
+        product(3)
+        largest(1, whole)
+        largest(2, whole)
+        exp_sum_gpsimd(1)
+        e2 = exp_vector(2, whole)
+        largest(3, halves)
+        e3 = exp_vector(3, halves)
+        for u in range(2):
+            sum_vector(2, e2, u)
+        for u in range(2):
+            sum_vector(3, e3, u)
+        for t in range(PACK):
+            nc.tensor.transpose(top_d[:, t, :], top_sb[:, t, :], ident[:])
+        for t in range(PACK):
+            nc.tensor.transpose(sum_d[:, t, :], sum_sb[t // 2][:, t % 2, :], ident[:])
 
         VH = V // 2
         logs = [keep.tile([P, PACK, VH], F32, name="logs%d" % g) for g in range(2)]

@@ -73,16 +73,12 @@ def tile_picked_lsep_none_po_kernel(tc, x_words, x_scales, w1, offs, out_0, out_
                 nc.vector.tensor_reduce(top_sb[:, a:b, c * LC : (c + 1) * LC], scores[:, a:b, :, :], AX.X, ALU.max)
 
         def exp_sum_gpsimd(c):
-            z = keep.tile([P, D, PACK, LC], F32, name="z%d" % c, tag="w_bf2" if c == 0 else "z%d" % c, align_bytes=64)
+            z = keep.tile([P, D, PACK, LC], F32, name="z%d" % c)
             e = keep.tile([P, D, PACK, LC], F32, name="e%d" % c)
-            pair = keep.tile([P, 2, PACK, LC], F32, name="pair%d" % c)
             shift = top_sb[:, :, c * LC : (c + 1) * LC].unsqueeze(1).to_broadcast([P, D, PACK, LC])
             nc.vector.tensor_tensor(z[:], y[c][:].rearrange("p (d i t) -> p d t i", d=D, t=PACK), shift, ALU.subtract)
             nc.scalar.activation(e[:], z[:], ACT.Exp)
-            nc.gpsimd.tensor_tensor(pair[:], e[:, 0:2, :, :], e[:, 2:4, :, :], ALU.add)
-            for u in range(2):
-                nc.gpsimd.tensor_tensor(sum_sb[u][:, :, c * LC : (c + 1) * LC], pair[:, 0, 2 * u : 2 * u + 2, :],
-                                        pair[:, 1, 2 * u : 2 * u + 2, :], ALU.add)
+            nc.gpsimd.tensor_tensor(pair[:, :, :, c * LC : (c + 1) * LC], e[:, 0:2, :, :], e[:, 2:4, :, :], ALU.add)
 
         def exp_vector(c, pieces):
             z = keep.tile([P, PACK, LC, D], F32, name="z%d" % c)
@@ -98,6 +94,7 @@ def tile_picked_lsep_none_po_kernel(tc, x_words, x_scales, w1, offs, out_0, out_
             nc.vector.tensor_reduce(sum_sb[u][:, :, c * LC : (c + 1) * LC], e[:, 2 * u : 2 * u + 2, :, :], AX.X, ALU.add)
 
         sum_sb = [keep.tile([P, 2, P], F32, name="sum_sb%d" % u) for u in range(2)]
+        pair = keep.tile([P, 2, PACK, 2 * LC], F32, name="pair")
         whole, halves = ((0, PACK),), ((0, 2), (2, PACK))
         top_d = psum.tile([P, PACK, V], F32, name="top_d")
         sum_d = psum.tile([P, PACK, V], F32, name="sum_d")
@@ -120,6 +117,9 @@ def tile_picked_lsep_none_po_kernel(tc, x_words, x_scales, w1, offs, out_0, out_
         largest(1, whole)
         largest(2, whole)
         exp_sum_gpsimd(1)
+        for u in range(2):
+            nc.gpsimd.tensor_tensor(sum_sb[u][:, :, 0 : 2 * LC], pair[:, 0, 2 * u : 2 * u + 2, :],
+                                    pair[:, 1, 2 * u : 2 * u + 2, :], ALU.add)
         e2 = exp_vector(2, whole)
         largest(3, halves)
         e3 = exp_vector(3, halves)
@@ -133,24 +133,27 @@ def tile_picked_lsep_none_po_kernel(tc, x_words, x_scales, w1, offs, out_0, out_
             nc.tensor.transpose(sum_d[:, t, :], sum_sb[t // 2][:, t % 2, :], ident[:])
 
         VH = V // 2
-        logs = [keep.tile([P, PACK, VH], F32, name="logs%d" % g) for g in range(2)]
+        pieces = ((0, VH), (VH, VH + VH // 2), (VH + VH // 2, V))
         res = keep.tile([P, PACK, V], F32, name="res")
-        res_bf = [keep.tile([P, VH, PACK], BF16, name="res_bf%d" % g, align_bytes=64) for g in range(2)]
+        res_bf = keep.tile([P, V, PACK], BF16, name="res_bf", align_bytes=64)
         oq = keep.tile([P, V], U32, name="oq", align_bytes=64)
         osc = keep.tile([P, V], U8, name="osc", align_bytes=64)
-        for g in range(2):
-            cols = slice(g * VH, (g + 1) * VH)
-            nc.scalar.activation(logs[g][:], sum_d[:, :, cols], ACT.Ln)
-            nc.vector.tensor_tensor(res[:, :, cols], top_d[:, :, cols], logs[g][:], ALU.add)
+        for a, b in pieces:
+            logs = keep.tile([P, PACK, b - a], F32, name="logs%d" % a)
+            nc.scalar.activation(logs[:], sum_d[:, :, a:b], ACT.Ln)
+            nc.vector.tensor_tensor(res[:, :, a:b], top_d[:, :, a:b], logs[:], ALU.add)
         nc.sync.dma_start(out_0.rearrange("(p t) v -> p t v", t=PACK), res[:])
-        for g in range(2):
-            cols = slice(g * VH, (g + 1) * VH)
-            nc.scalar.activation(res_bf[g][:].rearrange("p (c i) t -> p c t i", i=4),
-                                 res[:, :, cols].rearrange("p t (c i) -> p c t i", i=4), ACT.Copy)
+        for a, b in pieces:
+            dst = res_bf[:, a:b, :].rearrange("p (c i) t -> p c t i", i=4)
+            src = res[:, :, a:b].rearrange("p t (c i) -> p c t i", i=4)
+            if b == V:
+                nc.vector.tensor_copy(dst, src)
+            else:
+                nc.scalar.activation(dst, src, ACT.Copy)
         for g in range(2):
             cols = slice(g * VH, (g + 1) * VH)
             nc.vector.quantize_mx(out=oq[:, cols].bitcast(FP8X4), scales=osc[:, cols],
-                                  in_=res_bf[g][:].rearrange("p v t -> p (v t)"))
+                                  in_=res_bf[:, cols, :].rearrange("p v t -> p (v t)"))
         nc.sync.dma_start(out_1[0].rearrange("p c r -> p (c r)").bitcast(I32), oq[:].bitcast(I32))
         for q in range(4):
             eng = nc.scalar if q % 2 == 0 else nc.sync

from contextlib import ExitStack

import concourse.mybir as mybir
from concourse.masks import make_identity

F32 = mybir.dt.float32
BF16 = mybir.dt.bfloat16
I32 = mybir.dt.int32
U32 = mybir.dt.uint32
U16 = mybir.dt.uint16
U8 = mybir.dt.uint8
FP8X4 = mybir.dt.float8_e4m3fn_x4
ACT = mybir.ActivationFunctionType
ALU = mybir.AluOpType
AX = mybir.AxisListType

K, T, S, V, N = 512, 1024, 512, 128, 512
D = S // V
P = 128
PACK = 4
FLOPS = 2 * K * S * N


def tile_picked_lsep_none_po_kernel(tc, x_words, x_scales, w1, offs, out_0, out_1, out_2):
    nc = tc.nc
    C = N // P
    with ExitStack() as ctx:
        keep = ctx.enter_context(tc.tile_pool(name="keep", bufs=1))
        psum = ctx.enter_context(tc.psum_pool(name="psum", bufs=1))

        offsets = keep.tile([P, S // 16], U16, name="offsets")
        xw = keep.tile([P, T], I32, name="xw", align_bytes=64)
        xs = keep.tile([P, T], U8, name="xs", align_bytes=64)
        nc.vector.memset(xs[:].bitcast(I32), 0)
        w_rows = w1.rearrange("(p j) m -> p j m", j=PACK)
        w_raw = [keep.tile([P, PACK, P], F32, name="w_raw%d" % c) for c in range(C)]
        nc.sync.dma_start(offsets[:], offs)
        nc.sync.dma_start(w_raw[0][:], w_rows[:, :, 0:P])
        for q in range(4):
            eng = nc.sync if q % 2 == 0 else nc.scalar
            eng.dma_start(xs[32 * q : 32 * q + 4, :].bitcast(I32), x_scales[0, 4 * q : 4 * q + 4, :].bitcast(I32))
        nc.sync.dma_start(xw[:], x_words[0].rearrange("p c r -> p (c r)").bitcast(I32))
        for c in range(1, C):
            nc.sync.dma_start(w_raw[c][:], w_rows[:, :, c * P : (c + 1) * P])
        ident = keep.tile([P, P], F32, name="ident")
        make_identity(nc, ident[:])

        gs = keep.tile([P, S], U8, name="gs", align_bytes=64)
        nc.vector.tensor_copy(gs[:], xs[:].indirect(offsets[:]))
        w_bf = [keep.tile([P, P, PACK], BF16, name="w_bf%d" % c, tag="w_bf%d" % c, align_bytes=64) for c in range(C)]
        wq = [keep.tile([P, P], U32, name="wq%d" % c, align_bytes=64) for c in range(C)]
        ws = [keep.tile([P, P], U8, name="ws%d" % c, align_bytes=64) for c in range(C)]
        y = [psum.tile([P, S], F32, name="y%d" % c, tag="y%d" % c) for c in range(C)]
        LC = P // PACK

        def cast(c):
            nc.scalar.activation(w_bf[c][:].rearrange("p (a i) j -> p a j i", i=4),
                                 w_raw[c][:].rearrange("p j (a i) -> p a j i", i=4), ACT.Copy)

        def quantise(c):
            nc.vector.quantize_mx(out=wq[c][:].bitcast(FP8X4), scales=ws[c][:],
                                  in_=w_bf[c][:].rearrange("p m j -> p (m j)"))

        def product(c):
            for d in range(D):
                cols = slice(d * V, (d + 1) * V)
                nc.tensor.matmul_mx(out=y[c][:, cols], lhsT=gw[:, cols].bitcast(FP8X4), lhsT_scale=gs[:, cols],
                                    rhs=wq[c][:].bitcast(FP8X4), rhs_scale=ws[c][:], start=True, stop=True)

        def largest(c, pieces):
            scores = y[c][:].rearrange("p (d i t) -> p t i d", d=D, t=PACK)
            for a, b in pieces:
                nc.vector.tensor_reduce(top_sb[:, a:b, c * LC : (c + 1) * LC], scores[:, a:b, :, :], AX.X, ALU.max)

        def exp_sum_gpsimd(c):
            z = keep.tile([P, D, PACK, LC], F32, name="z%d" % c)
            e = keep.tile([P, D, PACK, LC], F32, name="e%d" % c)
            shift = top_sb[:, :, c * LC : (c + 1) * LC].unsqueeze(1).to_broadcast([P, D, PACK, LC])
            nc.vector.tensor_tensor(z[:], y[c][:].rearrange("p (d i t) -> p d t i", d=D, t=PACK), shift, ALU.subtract)
            nc.scalar.activation(e[:], z[:], ACT.Exp)
            nc.gpsimd.tensor_tensor(pair[:, :, :, c * LC : (c + 1) * LC], e[:, 0:2, :, :], e[:, 2:4, :, :], ALU.add)

        def exp_vector(c, pieces):
            z = keep.tile([P, PACK, LC, D], F32, name="z%d" % c)
            e = keep.tile([P, PACK, LC, D], F32, name="e%d" % c)
            scores = y[c][:].rearrange("p (d i t) -> p t i d", d=D, t=PACK)
            for a, b in pieces:
                shift = top_sb[:, a:b, c * LC : (c + 1) * LC].unsqueeze(3).to_broadcast([P, b - a, LC, D])
                nc.vector.tensor_tensor(z[:, a:b, :, :], scores[:, a:b, :, :], shift, ALU.subtract)
                nc.scalar.activation(e[:, a:b, :, :], z[:, a:b, :, :], ACT.Exp)
            return e

        def sum_vector(c, e, u):
            nc.vector.tensor_reduce(sum_sb[u][:, :, c * LC : (c + 1) * LC], e[:, 2 * u : 2 * u + 2, :, :], AX.X, ALU.add)

        sum_sb = [keep.tile([P, 2, P], F32, name="sum_sb%d" % u) for u in range(2)]
        pair = keep.tile([P, 2, PACK, 2 * LC], F32, name="pair")
        whole, halves = ((0, PACK),), ((0, 2), (2, PACK))
        top_d = psum.tile([P, PACK, V], F32, name="top_d")
        sum_d = psum.tile([P, PACK, V], F32, name="sum_d")
        for c in range(C):
            cast(c)
        quantise(0)
        gw = keep.tile([P, S], U32, name="gw", align_bytes=64)
        for a, b in ((0, 2 * V), (2 * V, 3 * V), (3 * V, S)):
            nc.vector.tensor_copy(gw[:, a:b], xw[:].bitcast(U32).indirect(offsets[:, a // 16 : b // 16]))
        product(0)
        quantise(1)
        product(1)
        top_sb = keep.tile([P, PACK, P], F32, name="top_sb", tag="w_bf1", align_bytes=64)
        largest(0, whole)
        quantise(2)
        product(2)
        exp_sum_gpsimd(0)
        quantise(3)
        product(3)
        largest(1, whole)
        largest(2, whole)
        exp_sum_gpsimd(1)
        for u in range(2):
            nc.gpsimd.tensor_tensor(sum_sb[u][:, :, 0 : 2 * LC], pair[:, 0, 2 * u : 2 * u + 2, :],
                                    pair[:, 1, 2 * u : 2 * u + 2, :], ALU.add)
        e2 = exp_vector(2, whole)
        largest(3, halves)
        e3 = exp_vector(3, halves)
        for u in range(2):
            sum_vector(2, e2, u)
        for u in range(2):
            sum_vector(3, e3, u)
        for t in range(PACK):
            nc.tensor.transpose(top_d[:, t, :], top_sb[:, t, :], ident[:])
        for t in range(PACK):
            nc.tensor.transpose(sum_d[:, t, :], sum_sb[t // 2][:, t % 2, :], ident[:])

        VH = V // 2
        pieces = ((0, VH), (VH, VH + VH // 2), (VH + VH // 2, V))
        res = keep.tile([P, PACK, V], F32, name="res")
        res_bf = keep.tile([P, V, PACK], BF16, name="res_bf", align_bytes=64)
        oq = keep.tile([P, V], U32, name="oq", align_bytes=64)
        osc = keep.tile([P, V], U8, name="osc", align_bytes=64)
        for a, b in pieces:
            logs = keep.tile([P, PACK, b - a], F32, name="logs%d" % a)
            nc.scalar.activation(logs[:], sum_d[:, :, a:b], ACT.Ln)
            nc.vector.tensor_tensor(res[:, :, a:b], top_d[:, :, a:b], logs[:], ALU.add)
        nc.sync.dma_start(out_0.rearrange("(p t) v -> p t v", t=PACK), res[:])
        for a, b in pieces:
            dst = res_bf[:, a:b, :].rearrange("p (c i) t -> p c t i", i=4)
            src = res[:, :, a:b].rearrange("p t (c i) -> p c t i", i=4)
            if b == V:
                nc.vector.tensor_copy(dst, src)
            else:
                nc.scalar.activation(dst, src, ACT.Copy)
        for g in range(2):
            cols = slice(g * VH, (g + 1) * VH)
            nc.vector.quantize_mx(out=oq[:, cols].bitcast(FP8X4), scales=osc[:, cols],
                                  in_=res_bf[:, cols, :].rearrange("p v t -> p (v t)"))
        nc.sync.dma_start(out_1[0].rearrange("p c r -> p (c r)").bitcast(I32), oq[:].bitcast(I32))
        for q in range(4):
            eng = nc.scalar if q % 2 == 0 else nc.sync
            eng.dma_start(out_2[0, 4 * q : 4 * q + 4, :].bitcast(I32), osc[32 * q : 32 * q + 4, :].bitcast(I32))
